import numpy as np
import ml_dtypes


def mxq(x, axis, fmt="e4m3"):
    dtype, down = {"e4m3": (ml_dtypes.float8_e4m3fn, 7), "e5m2": (ml_dtypes.float8_e5m2, 14)}[fmt]
    v = np.moveaxis(np.asarray(x, np.float32).astype(ml_dtypes.bfloat16).astype(np.float64), axis, -1)
    blocks = v.reshape(v.shape[:-1] + (-1, 32))
    amax = np.abs(blocks).max(-1, keepdims=True)
    byte = np.maximum(np.where(amax > 0, np.frexp(amax)[1] - 1 + 127, 0) - down, 1)
    scale = np.exp2(byte - 127.0)
    codes = (blocks / scale).astype(np.float32).astype(dtype).astype(np.float64)
    return np.moveaxis((codes * scale).reshape(v.shape), -1, axis)


WIDE = False


def mx_kscale(k):
    if not WIDE:
        return np.ones(k)
    levels = np.array([10, -10, 5, -5, 0])
    if k % 512:
        return np.exp2(np.random.permutation(np.resize(levels, k // 32))).repeat(32)
    a = np.empty((k // 512, 16))
    for p in range(k // 512):
        a[p, :8] = np.random.permutation(np.resize(levels, 8))
        for g in range(8):
            far = levels[np.abs(levels - a[p, g]) >= 10]
            a[p, g + 8] = far[np.random.randint(len(far))]
    return np.exp2(a.ravel()).repeat(32)


def f64(x):
    return np.asarray(x).astype(np.float64)


def striped(idx):
    return np.tile(idx.reshape(-1, 16).T, (8, 1)).astype(np.uint16)


def unstriped(offs):
    return offs[:16].T.reshape(-1).astype(np.int64)


E2M1 = np.array([0.0, 0.5, 1.0, 1.5, 2.0, 3.0, 4.0, 6.0, -0.0, -0.5, -1.0, -1.5, -2.0, -3.0, -4.0, -6.0])


def pack_weight(w, fmt):
    k, n = w.shape
    w = f64(np.asarray(w, np.float32).astype(ml_dtypes.bfloat16)).reshape(k // 32, 32, n)
    amax = np.abs(w).max(1)
    if fmt == "e4m3":
        byte = np.frexp(amax)[1] - 1 + 127 - 7
    else:
        mant, ex = np.frexp(amax / 6.0)
        byte = np.where(mant > 0.5, ex, ex - 1) + 127
    byte = np.clip(np.where(amax > 0, byte, 1), 1, 254)
    scaled = (w * np.exp2(127.0 - byte)[:, None, :]).reshape(k, n).astype(np.float32)
    by_word = np.ascontiguousarray(scaled.reshape(k // 512, 128, 4, n).transpose(0, 1, 3, 2))
    if fmt == "e4m3":
        words = by_word.astype(ml_dtypes.float8_e4m3fn).view(np.uint8)
    else:
        c = by_word.astype(ml_dtypes.float4_e2m1fn).view(np.uint8) & 0xF
        words = (c[..., 0::2] | (c[..., 1::2] << 4)).reshape(k // 512, 128, 2 * n)
    return np.ascontiguousarray(words), np.ascontiguousarray(byte.astype(np.uint8).reshape(k // 512, 16, n))


def unpack_weight(words, scales, fmt):
    g, _, n = scales.shape
    words = np.ascontiguousarray(words).reshape(g, 128, n, -1)
    if fmt == "e4m3":
        vals = words.view(ml_dtypes.float8_e4m3fn).astype(np.float64)
    else:
        nib = np.empty((g, 128, n, 4), np.uint8)
        nib[..., 0::2] = words & 0xF
        nib[..., 1::2] = words >> 4
        vals = E2M1[nib]
    vals = vals * np.repeat(np.exp2(scales.astype(np.float64) - 127.0), 8, axis=1)[..., None]
    return vals.transpose(0, 1, 3, 2).reshape(g * 512, n)


def sigmoid(v):
    return 1.0 / (1.0 + np.exp(-np.maximum(v, -700.0)))


K, T, E, H, N = 512, 640, 8, 512, 384
COUNTS = (128, 128, 128, 128, 128, 128, 128, 384)
STARTS = np.cumsum((0,) + COUNTS)


def by_expert(wq, xq):
    return np.concatenate([wq[e].T @ xq[:, STARTS[e]:STARTS[e + 1]] for e in range(E)], axis=1)


def setup_inputs():
    n = np.random.standard_normal
    s = mx_kscale(K)[:, None]
    u = mx_kscale(H)
    both = np.repeat(np.arange(E), COUNTS)
    pair = np.stack([both[:T], both[T:]])[:, np.random.permutation(T)]
    pair = np.where(np.random.rand(T) < 0.5, pair, pair[::-1])
    order = np.argsort(pair.reshape(-1), kind="stable")
    slot_token = order % T; pos = np.empty(2 * T, np.int64); pos[order] = np.arange(2 * T); pos = pos.reshape(2, T)
    g = np.random.uniform(0.2, 0.8, T)
    w1 = [pack_weight(m, "e2m1") for m in n((E, K, H)) / np.sqrt(K) / s[None]]
    w3 = [pack_weight(m, "e2m1") for m in n((E, K, H)) / np.sqrt(K) / s[None] * u[None, None, :]]
    w2 = [pack_weight(m, "e2m1") for m in n((E, H, N)) / np.sqrt(H) / u[None, :, None]]
    return {
        "xT": (n((K, T)) * s).astype(np.float32),
        "w1_words": np.stack([m[0] for m in w1]),
        "w1_scales": np.stack([m[1] for m in w1]),
        "w3_words": np.stack([m[0] for m in w3]),
        "w3_scales": np.stack([m[1] for m in w3]),
        "w2_words": np.stack([m[0] for m in w2]),
        "w2_scales": np.stack([m[1] for m in w2]),
        "gate": np.stack([np.tile(g, (N, 1)), np.tile(1.0 - g, (N, 1))]).astype(np.float32),
        "offs": striped(slot_token),
        "pos1": striped(pos[0]),
        "pos2": striped(pos[1]),
    }


def reference(xT, w1_words, w1_scales, w3_words, w3_scales, w2_words, w2_scales, gate, offs, pos1, pos2):
    idx = unstriped(offs)
    w1 = np.stack([unpack_weight(w1_words[e], w1_scales[e], "e2m1") for e in range(E)])
    w3 = np.stack([unpack_weight(w3_words[e], w3_scales[e], "e2m1") for e in range(E)])
    w2 = np.stack([unpack_weight(w2_words[e], w2_scales[e], "e2m1") for e in range(E)])
    xq = mxq(f64(xT)[:, idx], 0, "e4m3")
    h = sigmoid(by_expert(w1, xq))
    h = h * by_expert(w3, xq)
    y = by_expert(w2, mxq(h, 0, "e4m3"))
    return f64(gate[0]) * y[:, unstriped(pos1)] + f64(gate[1]) * y[:, unstriped(pos2)]

@@ -1,0 +1,213 @@
+from contextlib import ExitStack
+
+import concourse.mybir as mybir
+from concourse.masks import make_identity
+
+K, T, E, H, N = 512, 640, 8, 512, 384
+P = 128
+S = 2 * T
+FLOPS = 2 * S * (2 * K * H + H * N)
+
+F32 = mybir.dt.float32
+BF16 = mybir.dt.bfloat16
+I32 = mybir.dt.int32
+U32 = mybir.dt.uint32
+U16 = mybir.dt.uint16
+U8 = mybir.dt.uint8
+FP8 = mybir.dt.float8_e4m3fn_x4
+FP4 = mybir.dt.float4_e2m1fn_x4
+MULT = mybir.AluOpType.mult
+SIGMOID = mybir.ActivationFunctionType.Sigmoid
+
+G = S // P
+EXPERT_OF = [min(g, E - 1) for g in range(G)]
+
+
+def tile_moe_rag_glu_sigmoid_kernel(
+    tc, xT, w1_words, w1_scales, w3_words, w3_scales, w2_words, w2_scales, gate, offs, pos1, pos2, out
+):
+    nc = tc.nc
+    with ExitStack() as ctx:
+        keep = ctx.enter_context(tc.tile_pool(name="keep", bufs=1))
+        gath = ctx.enter_context(tc.tile_pool(name="gath", bufs=7))
+        work = ctx.enter_context(tc.tile_pool(name="work", bufs=3))
+        psum = ctx.enter_context(tc.psum_pool(name="psum", bufs=2))
+
+        offs_t = keep.tile([P, S // 16], U16, name="offs_t")
+        pos1_t = keep.tile([P, T // 16], U16, name="pos1_t")
+        pos2_t = keep.tile([P, T // 16], U16, name="pos2_t")
+        x_raw = keep.tile([P, 4, T], F32, name="x_raw")
+        x_grp = keep.tile([P, T, 4], BF16, align_bytes=64, name="x_grp")
+        x_codes = keep.tile([P, T], U32, align_bytes=64, name="x_codes")
+        x_scales = keep.tile([P, T], U8, align_bytes=64, name="x_scales")
+        w1_t = keep.tile([P, E, 2 * H], U8, align_bytes=64, name="w1_t")
+        w3_t = keep.tile([P, E, 2 * H], U8, align_bytes=64, name="w3_t")
+        w2_t = keep.tile([P, E, 2 * N], U8, align_bytes=64, name="w2_t")
+        s1_t = keep.tile([P, E, H], U8, align_bytes=64, name="s1_t")
+        s3_t = keep.tile([P, E, H], U8, align_bytes=64, name="s3_t")
+        s2_t = keep.tile([P, E, N], U8, align_bytes=64, name="s2_t")
+        gate_t = [keep.tile([P, 3, T], F32, name=f"gate_{c}") for c in range(2)]
+        y_t = [keep.tile([P, S], F32, name=f"y_{n}") for n in range(3)]
+        ident = keep.tile([P, P], F32, name="ident")
+        dummy = keep.tile([P, 1], F32, name="dummy")
+
+        for plane in (s1_t, s2_t, s3_t):
+            nc.vector.memset(plane[:].rearrange("p e i -> p (e i)").bitcast(I32), 0)
+        nc.gpsimd.memset(dummy[:], 0.0)
+        nc.gpsimd.memset(x_scales[:].bitcast(I32), 0)
+        make_identity(nc, ident[:])
+        nc.scalar.activation(dummy[:], dummy[:], SIGMOID)
+
+        x_hbm = xT.rearrange("(p j) t -> p j t", j=4)
+        last = E - 1
+
+        def load_words(queue, tile, words, lo, hi):
+            queue.dma_start(
+                tile[:, lo:hi, :].bitcast(I32), words[lo:hi, 0, :, :].rearrange("e p b -> p e b").bitcast(I32)
+            )
+
+        def load_scales(queue, tile, scales):
+            for r in range(4):
+                queue.dma_start(
+                    tile[r:P:32, :, :].bitcast(I32), scales[:, 0, r:16:4, :].rearrange("e q i -> q e i").bitcast(I32)
+                )
+
+        nc.sync.dma_start(offs_t[:], offs)
+        nc.sync.dma_start(x_raw[:, :, 0:384], x_hbm[:, :, 0:384])
+        load_scales(nc.sync, s1_t, w1_scales)
+        nc.sync.dma_start(x_raw[:, :, 384:T], x_hbm[:, :, 384:T])
+        load_words(nc.sync, w1_t, w1_words, last, E)
+        load_words(nc.sync, w3_t, w3_words, last, E)
+        load_scales(nc.sync, s3_t, w3_scales)
+        load_words(nc.sync, w2_t, w2_words, last, E)
+        load_scales(nc.sync, s2_t, w2_scales)
+        for lo, hi in ((6, 7), (3, 6), (0, 3)):
+            for tile, words in ((w1_t, w1_words), (w3_t, w3_words), (w2_t, w2_words)):
+                load_words(nc.sync, tile, words, lo, hi)
+        nc.sync.dma_start(pos1_t[:], pos1)
+        nc.sync.dma_start(pos2_t[:], pos2)
+        for c in range(2):
+            nc.sync.dma_start(gate_t[c][:], gate[c].rearrange("(n p) t -> p n t", p=P))
+
+        def cast(copy, lo, hi):
+            copy(x_grp[:, lo:hi, :], x_raw[:, :, lo:hi].rearrange("p j t -> p t j"))
+
+        def quantise(lo, hi):
+            nc.vector.quantize_mx(
+                out=x_codes[:, lo:hi].bitcast(FP8),
+                scales=x_scales[:, lo:hi],
+                in_=x_grp[:, lo:hi, :].rearrange("p t j -> p (t j)"),
+            )
+
+        cast(nc.scalar.copy, 256, 384)
+        cast(nc.vector.tensor_copy, 0, 256)
+        quantise(0, 256)
+        quantise(256, 384)
+        cast(nc.scalar.copy, 560, 640)
+        cast(nc.vector.tensor_copy, 384, 560)
+        quantise(384, 640)
+
+        slot_codes, slot_scales = {}, {}
+
+        def gather(first, count):
+            lists = offs_t[:, 8 * first : 8 * (first + count)]
+            codes = gath.tile([P, P * count], U32, align_bytes=64, name=f"gc{count}")
+            scales = gath.tile([P, P * count], U8, align_bytes=64, name=f"gs{count}")
+            nc.vector.tensor_copy(codes[:], x_codes[:].indirect(lists))
+            nc.vector.tensor_copy(scales[:], x_scales[:].indirect(lists))
+            for i in range(count):
+                slot_codes[first + i] = codes[:, P * i : P * (i + 1)]
+                slot_scales[first + i] = scales[:, P * i : P * (i + 1)]
+
+        ab = {}
+
+        def up(g):
+            e = EXPERT_OF[g]
+            a = psum.tile([P, H], F32, name="a")
+            b = psum.tile([P, H], F32, name="b")
+            for bank, words, scales in ((a, w1_t, s1_t), (b, w3_t, s3_t)):
+                nc.tensor.matmul_mx(
+                    out=bank[:],
+                    lhsT=slot_codes[g].bitcast(FP8),
+                    lhsT_scale=slot_scales[g],
+                    rhs=words[:, e, :].bitcast(FP4),
+                    rhs_scale=scales[:, e, :],
+                    start=True,
+                    stop=True,
+                )
+            ab[g] = (a, b)
+
+        h_t = {}
+
+        def act(g):
+            a, b = ab[g]
+            sig = work.tile([P, H], F32, name="sig")
+            h = work.tile([P, H], BF16, name="h")
+            nc.scalar.activation(sig[:], a[:], SIGMOID)
+            nc.vector.tensor_tensor(h[:], b[:], sig[:], MULT)
+            h_t[g] = h
+
+        grp = {}
+
+        def turn(g):
+            words = h_t[g][:].bitcast(F32)
+            xt = psum.tile([P, 2, P], F32, name="xt")
+            for u in range(2):
+                nc.tensor.transpose(xt[:, u, :], words[:, u : H // 2 : 2], ident[:])
+            hg = work.tile([P, P * 4], BF16, align_bytes=64, name="hg")
+            nc.scalar.copy(hg[:].bitcast(F32).rearrange("p (s u) -> p s u", u=2), xt[:].rearrange("p u s -> p s u"))
+            grp[g] = hg
+
+        hq = {}
+
+        def quant(g):
+            codes = work.tile([P, P], U32, align_bytes=64, name="hcodes")
+            scales = work.tile([P, P], U8, align_bytes=64, name="hscales")
+            nc.vector.quantize_mx(out=codes[:].bitcast(FP8), scales=scales[:], in_=grp[g][:])
+            hq[g] = (codes, scales)
+
+        def down(g):
+            e = EXPERT_OF[g]
+            codes, scales = hq[g]
+            y = psum.tile([P, 3, P], F32, name="y")
+            for n in range(3):
+                nc.tensor.matmul_mx(
+                    out=y[:, n, :],
+                    lhsT=w2_t[:, e, 256 * n : 256 * (n + 1)].bitcast(FP4),
+                    lhsT_scale=s2_t[:, e, P * n : P * (n + 1)],
+                    rhs=codes[:].bitcast(FP8),
+                    rhs_scale=scales[:],
+                    start=True,
+                    stop=True,
+                )
+            for n in range(3):
+                copy = nc.vector.tensor_copy if (g == 0 and n == 0) else nc.scalar.copy
+                copy(y_t[n][:, P * g : P * (g + 1)], y[:, n, :])
+
+        order = list(range(G - 1, -1, -1))
+        gather(G - 1, 1)
+        up(order[0])
+        gather(G - 2, 1)
+        for s in range(G + 2):
+            if s + 1 < G:
+                up(order[s + 1])
+            if s < G:
+                act(order[s])
+            if 1 <= s <= G:
+                turn(order[s - 1])
+                quant(order[s - 1])
+            if s % 2 == 0 and s + 3 < G:
+                gather(order[s + 3], 2)
+            if s >= 2:
+                down(order[s - 2])
+
+        for n in range(3):
+            parts = []
+            for c, lists in enumerate((pos1_t, pos2_t)):
+                part = work.tile([P, T], F32, name=f"part{c}")
+                nc.vector.tensor_tensor(part[:], y_t[n][:].indirect(lists[:]), gate_t[c][:, n, :], MULT)
+                parts.append(part)
+            res = work.tile([P, T], F32, name="res")
+            for lo, hi in ((0, T),) if n < 2 else ((0, T // 2), (T // 2, T)):
+                nc.vector.tensor_add(res[:, lo:hi], parts[0][:, lo:hi], parts[1][:, lo:hi])
+                nc.sync.dma_start(out[P * n : P * (n + 1), lo:hi], res[:, lo:hi])

@@ -20,6 +20,8 @@ MULT = mybir.AluOpType.mult
 SIGMOID = mybir.ActivationFunctionType.Sigmoid
 
 G = S // P
+X_CUT = (0, 384, T)
+W_ROW = 2 * (H + H + N)
 EXPERT_OF = [min(g, E - 1) for g in range(G)]
 
 
@@ -29,6 +31,7 @@ def tile_moe_rag_glu_sigmoid_kernel(
     nc = tc.nc
     with ExitStack() as ctx:
         keep = ctx.enter_context(tc.tile_pool(name="keep", bufs=1))
+        early = ctx.enter_context(tc.tile_pool(name="early", bufs=1))
         gath = ctx.enter_context(tc.tile_pool(name="gath", bufs=7))
         work = ctx.enter_context(tc.tile_pool(name="work", bufs=3))
         psum = ctx.enter_context(tc.psum_pool(name="psum", bufs=2))
@@ -36,76 +39,85 @@ def tile_moe_rag_glu_sigmoid_kernel(
         offs_t = keep.tile([P, S // 16], U16, name="offs_t")
         pos1_t = keep.tile([P, T // 16], U16, name="pos1_t")
         pos2_t = keep.tile([P, T // 16], U16, name="pos2_t")
-        x_raw = keep.tile([P, 4, T], F32, name="x_raw")
-        x_grp = keep.tile([P, T, 4], BF16, align_bytes=64, name="x_grp")
+        x_raw = [early.tile([P, 4, X_CUT[c + 1] - X_CUT[c]], F32, align_bytes=64, name=f"x_raw{c}", tag=f"r{c}") for c in range(2)]
+        x_grp = [early.tile([P, X_CUT[c + 1] - X_CUT[c], 4], BF16, align_bytes=64, name=f"x_grp{c}", tag=f"g{c}") for c in range(2)]
         x_codes = keep.tile([P, T], U32, align_bytes=64, name="x_codes")
         x_scales = keep.tile([P, T], U8, align_bytes=64, name="x_scales")
-        w1_t = keep.tile([P, E, 2 * H], U8, align_bytes=64, name="w1_t")
-        w3_t = keep.tile([P, E, 2 * H], U8, align_bytes=64, name="w3_t")
-        w2_t = keep.tile([P, E, 2 * N], U8, align_bytes=64, name="w2_t")
         s1_t = keep.tile([P, E, H], U8, align_bytes=64, name="s1_t")
         s3_t = keep.tile([P, E, H], U8, align_bytes=64, name="s3_t")
         s2_t = keep.tile([P, E, N], U8, align_bytes=64, name="s2_t")
-        gate_t = [keep.tile([P, 3, T], F32, name=f"gate_{c}") for c in range(2)]
         y_t = [keep.tile([P, S], F32, name=f"y_{n}") for n in range(3)]
         ident = keep.tile([P, P], F32, name="ident")
-        dummy = keep.tile([P, 1], F32, name="dummy")
+        dummy = early.tile([P, 1], F32, align_bytes=64, name="dummy", tag="w")
 
-        for plane in (s1_t, s2_t, s3_t):
+        nc.gpsimd.memset(s1_t[:].rearrange("p e i -> p (e i)").bitcast(I32), 0)
+        nc.vector.memset(dummy[:], 0.0)
+        for plane in (s3_t, s2_t):
             nc.vector.memset(plane[:].rearrange("p e i -> p (e i)").bitcast(I32), 0)
-        nc.gpsimd.memset(dummy[:], 0.0)
+        nc.scalar.activation(dummy[:], dummy[:], SIGMOID)
         nc.gpsimd.memset(x_scales[:].bitcast(I32), 0)
         make_identity(nc, ident[:])
-        nc.scalar.activation(dummy[:], dummy[:], SIGMOID)
 
-        x_hbm = xT.rearrange("(p j) t -> p j t", j=4)
         last = E - 1
+        w_last = early.tile([P, 1, W_ROW], U8, align_bytes=64, name="w_last", tag="w")
+        w_hbm = ((0, w1_words), (2 * H, w3_words), (4 * H, w2_words))
 
-        def load_words(queue, tile, words, lo, hi):
+        def load_words(queue, tile, which, lo, hi, first):
+            at, words = w_hbm[which]
             queue.dma_start(
-                tile[:, lo:hi, :].bitcast(I32), words[lo:hi, 0, :, :].rearrange("e p b -> p e b").bitcast(I32)
+                tile[:, lo - first : hi - first, at : at + words.shape[3]].bitcast(I32),
+                words[lo:hi, 0, :, :].rearrange("e p b -> p e b").bitcast(I32),
             )
 
-        def load_scales(queue, tile, scales):
+        def load_scales(tile, scales):
             for r in range(4):
-                queue.dma_start(
+                nc.sync.dma_start(
                     tile[r:P:32, :, :].bitcast(I32), scales[:, 0, r:16:4, :].rearrange("e q i -> q e i").bitcast(I32)
                 )
 
+        x_hbm = xT.rearrange("(p j) t -> p j t", j=4)
+        for c in range(2):
+            nc.sync.dma_start(x_raw[c][:], x_hbm[:, :, X_CUT[c] : X_CUT[c + 1]])
         nc.sync.dma_start(offs_t[:], offs)
-        nc.sync.dma_start(x_raw[:, :, 0:384], x_hbm[:, :, 0:384])
-        load_scales(nc.sync, s1_t, w1_scales)
-        nc.sync.dma_start(x_raw[:, :, 384:T], x_hbm[:, :, 384:T])
-        load_words(nc.sync, w1_t, w1_words, last, E)
-        load_words(nc.sync, w3_t, w3_words, last, E)
-        load_scales(nc.sync, s3_t, w3_scales)
-        load_words(nc.sync, w2_t, w2_words, last, E)
-        load_scales(nc.sync, s2_t, w2_scales)
-        for lo, hi in ((6, 7), (3, 6), (0, 3)):
-            for tile, words in ((w1_t, w1_words), (w3_t, w3_words), (w2_t, w2_words)):
-                load_words(nc.sync, tile, words, lo, hi)
+        load_scales(s1_t, w1_scales)
+        for which in range(3):
+            load_words(nc.scalar, w_last, which, last, E, last)
+        load_scales(s3_t, w3_scales)
+        w1_rest = keep.tile([P, last, 2 * H], U8, align_bytes=64, name="w1_rest")
+        nc.gpsimd.dma_start(w1_rest[:].bitcast(I32), w1_words[0:last, 0, :, :].rearrange("e p b -> p e b").bitcast(I32))
+        load_scales(s2_t, w2_scales)
         nc.sync.dma_start(pos1_t[:], pos1)
         nc.sync.dma_start(pos2_t[:], pos2)
-        for c in range(2):
-            nc.sync.dma_start(gate_t[c][:], gate[c].rearrange("(n p) t -> p n t", p=P))
 
-        def cast(copy, lo, hi):
-            copy(x_grp[:, lo:hi, :], x_raw[:, :, lo:hi].rearrange("p j t -> p t j"))
+        for c, widths in enumerate(((256, 128), (256,))):
+            size = X_CUT[c + 1] - X_CUT[c]
+            for copy, lo, hi in ((nc.scalar.copy, size // 2, size), (nc.vector.tensor_copy, 0, size // 2)):
+                copy(x_grp[c][:, lo:hi, :], x_raw[c][:, :, lo:hi].rearrange("p j t -> p t j"))
+            lo = 0
+            for width in widths:
+                cols = slice(X_CUT[c] + lo, X_CUT[c] + lo + width)
+                nc.vector.quantize_mx(
+                    out=x_codes[:, cols].bitcast(FP8),
+                    scales=x_scales[:, cols],
+                    in_=x_grp[c][:, lo : lo + width, :].rearrange("p t j -> p (t j)"),
+                )
+                lo += width
 
-        def quantise(lo, hi):
-            nc.vector.quantize_mx(
-                out=x_codes[:, lo:hi].bitcast(FP8),
-                scales=x_scales[:, lo:hi],
-                in_=x_grp[:, lo:hi, :].rearrange("p t j -> p (t j)"),
+        w32_rest = early.tile([P, last, 2 * (H + N)], U8, align_bytes=64, name="w32_rest", tag="r1")
+        for at, words in ((0, w3_words), (2 * H, w2_words)):
+            nc.scalar.dma_start(
+                w32_rest[:, :, at : at + words.shape[3]].bitcast(I32),
+                words[0:last, 0, :, :].rearrange("e p b -> p e b").bitcast(I32),
             )
+        gate_t = early.tile([P, 2, 3, T], F32, align_bytes=64, name="gate_t", tag="g1")
+        nc.sync.dma_start(gate_t[:].rearrange("p c n t -> p (c n) t"), gate.rearrange("c (n p) t -> p (c n) t", p=P))
 
-        cast(nc.scalar.copy, 256, 384)
-        cast(nc.vector.tensor_copy, 0, 256)
-        quantise(0, 256)
-        quantise(256, 384)
-        cast(nc.scalar.copy, 560, 640)
-        cast(nc.vector.tensor_copy, 384, 560)
-        quantise(384, 640)
+        def words_of(e, lo, hi):
+            if e == last:
+                return w_last[:, 0, lo:hi].bitcast(FP4)
+            if hi <= 2 * H:
+                return w1_rest[:, e, lo:hi].bitcast(FP4)
+            return w32_rest[:, e, lo - 2 * H : hi - 2 * H].bitcast(FP4)
 
         slot_codes, slot_scales = {}, {}
 
@@ -125,12 +137,12 @@ def tile_moe_rag_glu_sigmoid_kernel(
             e = EXPERT_OF[g]
             a = psum.tile([P, H], F32, name="a")
             b = psum.tile([P, H], F32, name="b")
-            for bank, words, scales in ((a, w1_t, s1_t), (b, w3_t, s3_t)):
+            for bank, at, scales in ((a, 0, s1_t), (b, 2 * H, s3_t)):
                 nc.tensor.matmul_mx(
                     out=bank[:],
                     lhsT=slot_codes[g].bitcast(FP8),
                     lhsT_scale=slot_scales[g],
-                    rhs=words[:, e, :].bitcast(FP4),
+                    rhs=words_of(e, at, at + 2 * H),
                     rhs_scale=scales[:, e, :],
                     start=True,
                     stop=True,
@@ -155,7 +167,8 @@ def tile_moe_rag_glu_sigmoid_kernel(
             for u in range(2):
                 nc.tensor.transpose(xt[:, u, :], words[:, u : H // 2 : 2], ident[:])
             hg = work.tile([P, P * 4], BF16, align_bytes=64, name="hg")
-            nc.scalar.copy(hg[:].bitcast(F32).rearrange("p (s u) -> p s u", u=2), xt[:].rearrange("p u s -> p s u"))
+            copy = nc.vector.tensor_copy if g == 0 else nc.scalar.copy
+            copy(hg[:].bitcast(F32).rearrange("p (s u) -> p s u", u=2), xt[:].rearrange("p u s -> p s u"))
             grp[g] = hg
 
         hq = {}
@@ -173,7 +186,7 @@ def tile_moe_rag_glu_sigmoid_kernel(
             for n in range(3):
                 nc.tensor.matmul_mx(
                     out=y[:, n, :],
-                    lhsT=w2_t[:, e, 256 * n : 256 * (n + 1)].bitcast(FP4),
+                    lhsT=words_of(e, 4 * H + 2 * P * n, 4 * H + 2 * P * (n + 1)),
                     lhsT_scale=s2_t[:, e, P * n : P * (n + 1)],
                     rhs=codes[:].bitcast(FP8),
                     rhs_scale=scales[:],
@@ -181,7 +194,7 @@ def tile_moe_rag_glu_sigmoid_kernel(
                     stop=True,
                 )
             for n in range(3):
-                copy = nc.vector.tensor_copy if (g == 0 and n == 0) else nc.scalar.copy
+                copy = nc.vector.tensor_copy if (n == 0 and g in (0, 1, 3, 5)) else nc.scalar.copy
                 copy(y_t[n][:, P * g : P * (g + 1)], y[:, n, :])
 
         order = list(range(G - 1, -1, -1))
@@ -205,7 +218,7 @@ def tile_moe_rag_glu_sigmoid_kernel(
             parts = []
             for c, lists in enumerate((pos1_t, pos2_t)):
                 part = work.tile([P, T], F32, name=f"part{c}")
-                nc.vector.tensor_tensor(part[:], y_t[n][:].indirect(lists[:]), gate_t[c][:, n, :], MULT)
+                nc.vector.tensor_tensor(part[:], y_t[n][:].indirect(lists[:]), gate_t[:, c, n, :], MULT)
                 parts.append(part)
             res = work.tile([P, T], F32, name="res")
             for lo, hi in ((0, T),) if n < 2 else ((0, T // 2), (T // 2, T)):

@@ -80,9 +80,10 @@ def tile_moe_rag_glu_sigmoid_kernel(
             nc.sync.dma_start(x_raw[c][:], x_hbm[:, :, X_CUT[c] : X_CUT[c + 1]])
         nc.sync.dma_start(offs_t[:], offs)
         load_scales(s1_t, w1_scales)
-        for which in range(3):
+        for which in range(2):
             load_words(nc.scalar, w_last, which, last, E, last)
         load_scales(s3_t, w3_scales)
+        load_words(nc.sync, w_last, 2, last, E, last)
         w1_rest = keep.tile([P, last, 2 * H], U8, align_bytes=64, name="w1_rest")
         nc.gpsimd.dma_start(w1_rest[:].bitcast(I32), w1_words[0:last, 0, :, :].rearrange("e p b -> p e b").bitcast(I32))
         load_scales(s2_t, w2_scales)
@@ -214,13 +215,27 @@ def tile_moe_rag_glu_sigmoid_kernel(
             if s >= 2:
                 down(order[s - 2])
 
-        for n in range(3):
-            parts = []
-            for c, lists in enumerate((pos1_t, pos2_t)):
-                part = work.tile([P, T], F32, name=f"part{c}")
-                nc.vector.tensor_tensor(part[:], y_t[n][:].indirect(lists[:]), gate_t[:, c, n, :], MULT)
-                parts.append(part)
-            res = work.tile([P, T], F32, name="res")
-            for lo, hi in ((0, T),) if n < 2 else ((0, T // 2), (T // 2, T)):
-                nc.vector.tensor_add(res[:, lo:hi], parts[0][:, lo:hi], parts[1][:, lo:hi])
-                nc.sync.dma_start(out[P * n : P * (n + 1), lo:hi], res[:, lo:hi])
+        parts = {}
+
+        def weigh(n, c, lo, hi):
+            if (n, c) not in parts:
+                parts[n, c] = work.tile([P, T], F32, name=f"part{c}")
+            lists = (pos1_t, pos2_t)[c][:, lo // 16 : hi // 16]
+            nc.vector.tensor_tensor(parts[n, c][:, lo:hi], y_t[n][:].indirect(lists), gate_t[:, c, n, lo:hi], MULT)
+
+        def add_up(n, lo, hi):
+            res = work.tile([P, hi - lo], F32, name=f"res{hi - lo}")
+            nc.vector.tensor_add(res[:], parts[n, 0][:, lo:hi], parts[n, 1][:, lo:hi])
+            nc.sync.dma_start(out[P * n : P * (n + 1), lo:hi], res[:])
+
+        weigh(0, 0, 0, T)
+        weigh(0, 1, 0, T)
+        weigh(1, 0, 0, T)
+        add_up(0, 0, T)
+        weigh(1, 1, 0, T)
+        weigh(2, 0, 0, T)
+        add_up(1, 0, T)
+        weigh(2, 1, 0, T // 2)
+        weigh(2, 1, T // 2, T)
+        add_up(2, 0, T // 2)
+        add_up(2, T // 2, T)

from contextlib import ExitStack

import concourse.mybir as mybir
from concourse.masks import make_identity

K, T, E, H, N = 512, 640, 8, 512, 384
P = 128
S = 2 * T
FLOPS = 2 * S * (2 * K * H + H * N)

F32 = mybir.dt.float32
BF16 = mybir.dt.bfloat16
I32 = mybir.dt.int32
U32 = mybir.dt.uint32
U16 = mybir.dt.uint16
U8 = mybir.dt.uint8
FP8 = mybir.dt.float8_e4m3fn_x4
FP4 = mybir.dt.float4_e2m1fn_x4
MULT = mybir.AluOpType.mult
SIGMOID = mybir.ActivationFunctionType.Sigmoid

G = S // P
X_CUT = (0, 384, T)
W_ROW = 2 * (H + H + N)
EXPERT_OF = [min(g, E - 1) for g in range(G)]


def tile_moe_rag_glu_sigmoid_kernel(
    tc, xT, w1_words, w1_scales, w3_words, w3_scales, w2_words, w2_scales, gate, offs, pos1, pos2, out
):
    nc = tc.nc
    with ExitStack() as ctx:
        keep = ctx.enter_context(tc.tile_pool(name="keep", bufs=1))
        early = ctx.enter_context(tc.tile_pool(name="early", bufs=1))
        gath = ctx.enter_context(tc.tile_pool(name="gath", bufs=7))
        work = ctx.enter_context(tc.tile_pool(name="work", bufs=3))
        psum = ctx.enter_context(tc.psum_pool(name="psum", bufs=2))

        offs_t = keep.tile([P, S // 16], U16, name="offs_t")
        pos1_t = keep.tile([P, T // 16], U16, name="pos1_t")
        pos2_t = keep.tile([P, T // 16], U16, name="pos2_t")
        x_raw = [early.tile([P, 4, X_CUT[c + 1] - X_CUT[c]], F32, align_bytes=64, name=f"x_raw{c}", tag=f"r{c}") for c in range(2)]
        x_grp = [early.tile([P, X_CUT[c + 1] - X_CUT[c], 4], BF16, align_bytes=64, name=f"x_grp{c}", tag=f"g{c}") for c in range(2)]
        x_codes = keep.tile([P, T], U32, align_bytes=64, name="x_codes")
        x_scales = keep.tile([P, T], U8, align_bytes=64, name="x_scales")
        s1_t = keep.tile([P, E, H], U8, align_bytes=64, name="s1_t")
        s3_t = keep.tile([P, E, H], U8, align_bytes=64, name="s3_t")
        s2_t = keep.tile([P, E, N], U8, align_bytes=64, name="s2_t")
        y_t = [keep.tile([P, S], F32, name=f"y_{n}") for n in range(3)]
        ident = keep.tile([P, P], F32, name="ident")
        dummy = early.tile([P, 1], F32, align_bytes=64, name="dummy", tag="w")

        nc.gpsimd.memset(s1_t[:].rearrange("p e i -> p (e i)").bitcast(I32), 0)
        nc.vector.memset(dummy[:], 0.0)
        for plane in (s3_t, s2_t):
            nc.vector.memset(plane[:].rearrange("p e i -> p (e i)").bitcast(I32), 0)
        nc.scalar.activation(dummy[:], dummy[:], SIGMOID)
        nc.gpsimd.memset(x_scales[:].bitcast(I32), 0)
        make_identity(nc, ident[:])

        last = E - 1
        w_last = early.tile([P, 1, W_ROW], U8, align_bytes=64, name="w_last", tag="w")
        w_hbm = ((0, w1_words), (2 * H, w3_words), (4 * H, w2_words))

        def load_words(queue, tile, which, lo, hi, first):
            at, words = w_hbm[which]
            queue.dma_start(
                tile[:, lo - first : hi - first, at : at + words.shape[3]].bitcast(I32),
                words[lo:hi, 0, :, :].rearrange("e p b -> p e b").bitcast(I32),
            )

        def load_scales(tile, scales):
            for r in range(4):
                nc.sync.dma_start(
                    tile[r:P:32, :, :].bitcast(I32), scales[:, 0, r:16:4, :].rearrange("e q i -> q e i").bitcast(I32)
                )

        x_hbm = xT.rearrange("(p j) t -> p j t", j=4)
        for c in range(2):
            nc.sync.dma_start(x_raw[c][:], x_hbm[:, :, X_CUT[c] : X_CUT[c + 1]])
        nc.sync.dma_start(offs_t[:], offs)
        load_scales(s1_t, w1_scales)
        for which in range(2):
            load_words(nc.scalar, w_last, which, last, E, last)
        load_scales(s3_t, w3_scales)
        load_words(nc.sync, w_last, 2, last, E, last)
        w1_rest = keep.tile([P, last, 2 * H], U8, align_bytes=64, name="w1_rest")
        nc.gpsimd.dma_start(w1_rest[:].bitcast(I32), w1_words[0:last, 0, :, :].rearrange("e p b -> p e b").bitcast(I32))
        load_scales(s2_t, w2_scales)
        nc.sync.dma_start(pos1_t[:], pos1)
        nc.sync.dma_start(pos2_t[:], pos2)

        for c, widths in enumerate(((256, 128), (256,))):
            size = X_CUT[c + 1] - X_CUT[c]
            for copy, lo, hi in ((nc.scalar.copy, size // 2, size), (nc.vector.tensor_copy, 0, size // 2)):
                copy(x_grp[c][:, lo:hi, :], x_raw[c][:, :, lo:hi].rearrange("p j t -> p t j"))
            lo = 0
            for width in widths:
                cols = slice(X_CUT[c] + lo, X_CUT[c] + lo + width)
                nc.vector.quantize_mx(
                    out=x_codes[:, cols].bitcast(FP8),
                    scales=x_scales[:, cols],
                    in_=x_grp[c][:, lo : lo + width, :].rearrange("p t j -> p (t j)"),
                )
                lo += width

        w32_rest = early.tile([P, last, 2 * (H + N)], U8, align_bytes=64, name="w32_rest", tag="r1")
        for at, words in ((0, w3_words), (2 * H, w2_words)):
            nc.scalar.dma_start(
                w32_rest[:, :, at : at + words.shape[3]].bitcast(I32),
                words[0:last, 0, :, :].rearrange("e p b -> p e b").bitcast(I32),
            )
        gate_t = early.tile([P, 2, 3, T], F32, align_bytes=64, name="gate_t", tag="g1")
        nc.sync.dma_start(gate_t[:].rearrange("p c n t -> p (c n) t"), gate.rearrange("c (n p) t -> p (c n) t", p=P))

        def words_of(e, lo, hi):
            if e == last:
                return w_last[:, 0, lo:hi].bitcast(FP4)
            if hi <= 2 * H:
                return w1_rest[:, e, lo:hi].bitcast(FP4)
            return w32_rest[:, e, lo - 2 * H : hi - 2 * H].bitcast(FP4)

        slot_codes, slot_scales = {}, {}

        def gather(first, count):
            lists = offs_t[:, 8 * first : 8 * (first + count)]
            codes = gath.tile([P, P * count], U32, align_bytes=64, name=f"gc{count}")
            scales = gath.tile([P, P * count], U8, align_bytes=64, name=f"gs{count}")
            nc.vector.tensor_copy(codes[:], x_codes[:].indirect(lists))
            nc.vector.tensor_copy(scales[:], x_scales[:].indirect(lists))
            for i in range(count):
                slot_codes[first + i] = codes[:, P * i : P * (i + 1)]
                slot_scales[first + i] = scales[:, P * i : P * (i + 1)]

        ab = {}

        def up(g):
            e = EXPERT_OF[g]
            a = psum.tile([P, H], F32, name="a")
            b = psum.tile([P, H], F32, name="b")
            for bank, at, scales in ((a, 0, s1_t), (b, 2 * H, s3_t)):
                nc.tensor.matmul_mx(
                    out=bank[:],
                    lhsT=slot_codes[g].bitcast(FP8),
                    lhsT_scale=slot_scales[g],
                    rhs=words_of(e, at, at + 2 * H),
                    rhs_scale=scales[:, e, :],
                    start=True,
                    stop=True,
                )
            ab[g] = (a, b)

        h_t = {}

        def act(g):
            a, b = ab[g]
            sig = work.tile([P, H], F32, name="sig")
            h = work.tile([P, H], BF16, name="h")
            nc.scalar.activation(sig[:], a[:], SIGMOID)
            nc.vector.tensor_tensor(h[:], b[:], sig[:], MULT)
            h_t[g] = h

        grp = {}

        def turn(g):
            words = h_t[g][:].bitcast(F32)
            xt = psum.tile([P, 2, P], F32, name="xt")
            for u in range(2):
                nc.tensor.transpose(xt[:, u, :], words[:, u : H // 2 : 2], ident[:])
            hg = work.tile([P, P * 4], BF16, align_bytes=64, name="hg")
            copy = nc.vector.tensor_copy if g == 0 else nc.scalar.copy
            copy(hg[:].bitcast(F32).rearrange("p (s u) -> p s u", u=2), xt[:].rearrange("p u s -> p s u"))
            grp[g] = hg

        hq = {}

        def quant(g):
            codes = work.tile([P, P], U32, align_bytes=64, name="hcodes")
            scales = work.tile([P, P], U8, align_bytes=64, name="hscales")
            nc.vector.quantize_mx(out=codes[:].bitcast(FP8), scales=scales[:], in_=grp[g][:])
            hq[g] = (codes, scales)

        def down(g):
            e = EXPERT_OF[g]
            codes, scales = hq[g]
            y = psum.tile([P, 3, P], F32, name="y")
            for n in range(3):
                nc.tensor.matmul_mx(
                    out=y[:, n, :],
                    lhsT=words_of(e, 4 * H + 2 * P * n, 4 * H + 2 * P * (n + 1)),
                    lhsT_scale=s2_t[:, e, P * n : P * (n + 1)],
                    rhs=codes[:].bitcast(FP8),
                    rhs_scale=scales[:],
                    start=True,
                    stop=True,
                )
            for n in range(3):
                copy = nc.vector.tensor_copy if (n == 0 and g in (0, 1, 3, 5)) else nc.scalar.copy
                copy(y_t[n][:, P * g : P * (g + 1)], y[:, n, :])

        order = list(range(G - 1, -1, -1))
        gather(G - 1, 1)
        up(order[0])
        gather(G - 2, 1)
        for s in range(G + 2):
            if s + 1 < G:
                up(order[s + 1])
            if s < G:
                act(order[s])
            if 1 <= s <= G:
                turn(order[s - 1])
                quant(order[s - 1])
            if s % 2 == 0 and s + 3 < G:
                gather(order[s + 3], 2)
            if s >= 2:
                down(order[s - 2])

        parts = {}

        def weigh(n, c, lo, hi):
            if (n, c) not in parts:
                parts[n, c] = work.tile([P, T], F32, name=f"part{c}")
            lists = (pos1_t, pos2_t)[c][:, lo // 16 : hi // 16]
            nc.vector.tensor_tensor(parts[n, c][:, lo:hi], y_t[n][:].indirect(lists), gate_t[:, c, n, lo:hi], MULT)

        def add_up(n, lo, hi):
            res = work.tile([P, hi - lo], F32, name=f"res{hi - lo}")
            nc.vector.tensor_add(res[:], parts[n, 0][:, lo:hi], parts[n, 1][:, lo:hi])
            nc.sync.dma_start(out[P * n : P * (n + 1), lo:hi], res[:])

        weigh(0, 0, 0, T)
        weigh(0, 1, 0, T)
        weigh(1, 0, 0, T)
        add_up(0, 0, T)
        weigh(1, 1, 0, T)
        weigh(2, 0, 0, T)
        add_up(1, 0, T)
        weigh(2, 1, 0, T // 2)
        weigh(2, 1, T // 2, T)
        add_up(2, 0, T // 2)
        add_up(2, T // 2, T)
